import numpy as np
import ml_dtypes


def mxq(x, axis, fmt="e4m3"):
    dtype, down = {"e4m3": (ml_dtypes.float8_e4m3fn, 7), "e5m2": (ml_dtypes.float8_e5m2, 14)}[fmt]
    v = np.moveaxis(np.asarray(x, np.float32).astype(ml_dtypes.bfloat16).astype(np.float64), axis, -1)
    blocks = v.reshape(v.shape[:-1] + (-1, 32))
    amax = np.abs(blocks).max(-1, keepdims=True)
    byte = np.maximum(np.where(amax > 0, np.frexp(amax)[1] - 1 + 127, 0) - down, 1)
    scale = np.exp2(byte - 127.0)
    codes = (blocks / scale).astype(np.float32).astype(dtype).astype(np.float64)
    return np.moveaxis((codes * scale).reshape(v.shape), -1, axis)


WIDE = False


def mx_kscale(k):
    if not WIDE:
        return np.ones(k)
    levels = np.array([10, -10, 5, -5, 0])
    if k % 512:
        return np.exp2(np.random.permutation(np.resize(levels, k // 32))).repeat(32)
    a = np.empty((k // 512, 16))
    for p in range(k // 512):
        a[p, :8] = np.random.permutation(np.resize(levels, 8))
        for g in range(8):
            far = levels[np.abs(levels - a[p, g]) >= 10]
            a[p, g + 8] = far[np.random.randint(len(far))]
    return np.exp2(a.ravel()).repeat(32)


def f64(x):
    return np.asarray(x).astype(np.float64)


def striped(idx):
    return np.tile(idx.reshape(-1, 16).T, (8, 1)).astype(np.uint16)


def unstriped(offs):
    return offs[:16].T.reshape(-1).astype(np.int64)


def pack_weight(w):
    k, n = w.shape
    w = f64(np.asarray(w, np.float32).astype(ml_dtypes.bfloat16)).reshape(k // 32, 32, n)
    amax = np.abs(w).max(1)
    byte = np.clip(np.where(amax > 0, np.frexp(amax)[1] - 1 + 127 - 7, 1), 1, 254)
    scaled = (w * np.exp2(127.0 - byte)[:, None, :]).reshape(k, n).astype(np.float32)
    words = np.ascontiguousarray(scaled.reshape(k // 512, 128, 4, n).transpose(0, 1, 3, 2)).astype(ml_dtypes.float8_e4m3fn).view(np.uint8)
    return words, np.ascontiguousarray(byte.astype(np.uint8).reshape(k // 512, 16, n))


def unpack_weight(words, scales):
    g, p, n, _ = words.shape
    vals = np.ascontiguousarray(words).view(ml_dtypes.float8_e4m3fn).astype(np.float64) * np.repeat(np.exp2(scales.astype(np.float64) - 127.0), 8, axis=1)[..., None]
    return vals.transpose(0, 1, 3, 2).reshape(g * 512, n)


def sigmoid(v):
    return 1.0 / (1.0 + np.exp(-np.maximum(v, -700.0)))


K, T, S, N = 512, 2048, 1024, 128
P = 2 ** 7


def setup_inputs():
    n = np.random.standard_normal
    s = mx_kscale(K)[:, None]
    packed_xT = pack_weight(n((K, T)) * s)
    return {
        "x_words": packed_xT[0],
        "x_scales": packed_xT[1],
        "w1": (n((K, N)) / np.sqrt(K) / s).astype(np.float32),
        "w2": (n((K, N)) / np.sqrt(K) / s).astype(np.float32),
        "paid": (np.random.uniform(0.3, 2.0, (N, S))).astype(np.float32),
        "wt": (np.tile(np.random.uniform(0.5, 1.5, S), (P, 1))).astype(np.float32),
        "offs": striped(np.random.permutation(T)[:S]),
    }


def reference(x_words, x_scales, w1, w2, paid, wt, offs):
    xq = unpack_weight(x_words, x_scales)[:, unstriped(offs)]
    yc = mxq(f64(w1), 0, "e4m3").T @ xq
    fac = 0.5 * (np.log(np.exp(yc) + 1.0)) + 1.0
    yp = mxq(f64(w2), 0, "e4m3").T @ xq
    cred = sigmoid(yp)
    fac2 = fac * (np.pad(fac, ((0, 0), (0, 1)))[:, 1:])
    fac4 = np.maximum(fac2, fac2 * (np.pad(fac2, ((0, 0), (0, 2)))[:, 2:]))
    ult = f64(paid) * fac4
    return ((np.pad(f64(paid), ((0, 0), (0, 1)))[:, 1:] - (f64(paid) * fac)) ** 2) * (f64(wt)[:1] / (f64(paid) + 0.2)) + cred * ult

@@ -1,0 +1,147 @@
+import math
+from contextlib import ExitStack
+
+import concourse.mybir as mybir
+
+K, T, S, M = 512, 2048, 1024, 128
+FLOPS = 2 * 2 * K * M * S
+
+F32 = mybir.dt.float32
+BF16 = mybir.dt.bfloat16
+I32 = mybir.dt.int32
+U32 = mybir.dt.uint32
+U16 = mybir.dt.uint16
+U8 = mybir.dt.uint8
+FP8X4 = mybir.dt.float8_e4m3fn_x4
+ALU = mybir.AluOpType
+ACT = mybir.ActivationFunctionType
+
+P = 128
+PACK = 4
+PIECE = 256
+HALF = 512
+PAD = 8
+LN_FLOOR = 2.0 ** -62
+
+
+def tile_picked_ychnld_err_p_kernel(tc, x_words, x_scales, w1, w2, paid, wt, offs, out):
+    nc = tc.nc
+    with ExitStack() as ctx:
+        sb = ctx.enter_context(tc.tile_pool(name="sb", bufs=1))
+        ps = ctx.enter_context(tc.psum_pool(name="ps", bufs=1))
+
+        offsets = sb.tile([P, S // 16], U16, name="offsets")
+        nc.sync.dma_start(offsets[:], offs)
+
+        xs = sb.tile([P, T], U8, name="xs", align_bytes=64)
+        nc.vector.memset(xs[:].bitcast(I32), 0)
+        for q in range(4):
+            nc.scalar.dma_start(out=xs[32 * q : 32 * q + 4, :].bitcast(I32), in_=x_scales[0, 4 * q : 4 * q + 4, :].bitcast(I32))
+
+        w_raw = []
+        for i, w in enumerate((w1, w2)):
+            raw = sb.tile([P, PACK, M], F32, name="w_raw%d" % i)
+            nc.sync.dma_start(out=raw[:], in_=w.rearrange("(p j) m -> p j m", j=PACK))
+            w_raw.append(raw)
+
+        xw = sb.tile([P, T], U32, name="xw", align_bytes=64)
+        nc.sync.dma_start(out=xw[:].bitcast(I32), in_=x_words[0].rearrange("p n t -> p (n t)").bitcast(I32))
+
+        pd = sb.tile([P, S + PAD], F32, name="pd")
+        nc.sync.dma_start(out=pd[:, :S], in_=paid)
+        wts = sb.tile([P, S], F32, name="wts")
+        nc.sync.dma_start(out=wts[:], in_=wt)
+
+        nc.vector.memset(pd[:, S:], 0.0)
+        half = sb.tile([P, 1], F32, name="half")
+        nc.scalar.activation(half[:], pd[:, S : S + 1], ACT.Sigmoid)
+
+        nf = sb.tile([P, S + PAD], F32, name="nf")
+        qq = sb.tile([P, S + PAD], F32, name="qq")
+        nc.vector.memset(nf[:, S:], 0.0)
+        nc.vector.memset(qq[:, S:], 0.0)
+
+        w_bf = sb.tile([P, 2, M, PACK], BF16, name="w_bf", align_bytes=64)
+        for i, sign in enumerate((-1.0, 1.0)):
+            nc.scalar.activation(w_bf[:, i], w_raw[i][:].rearrange("p j m -> p m j"), ACT.Copy, scale=sign)
+
+        gs = sb.tile([P, S], U8, name="gs", align_bytes=64)
+        for h in range(S // HALF):
+            nc.vector.tensor_copy(gs[:, h * HALF : (h + 1) * HALF], xs[:].indirect(offsets[:, h * HALF // 16 : (h + 1) * HALF // 16]))
+
+        w_codes = sb.tile([P, 2 * M], U32, name="w_codes", align_bytes=64)
+        w_scales = sb.tile([P, 2 * M], U8, name="w_scales", align_bytes=64)
+        nc.vector.quantize_mx(out=w_codes[:].bitcast(FP8X4), scales=w_scales[:], in_=w_bf[:].rearrange("p i m j -> p (i m j)"))
+
+        sg = sb.tile([P, 2, S + PAD], F32, name="sg")
+        acc = []
+        for c in range(S // PIECE):
+            cols = slice(c * PIECE, (c + 1) * PIECE)
+            gw = sb.tile([P, PIECE], U32, name="gw%d" % c, align_bytes=64)
+            nc.vector.tensor_copy(gw[:], xw[:].indirect(offsets[:, c * PIECE // 16 : (c + 1) * PIECE // 16]))
+            bank = ps.tile([P, 2, PIECE], F32, name="bank%d" % c)
+            for i in range(2):
+                nc.tensor.matmul_mx(
+                    out=bank[:, i, :],
+                    lhsT=w_codes[:, i * M : (i + 1) * M].bitcast(FP8X4),
+                    lhsT_scale=w_scales[:, i * M : (i + 1) * M],
+                    rhs=gw[:].bitcast(FP8X4),
+                    rhs_scale=gs[:, cols],
+                    start=True,
+                    stop=True,
+                )
+            nc.scalar.activation(sg[:, :, cols], bank[:], ACT.Sigmoid)
+            acc.append(bank)
+
+        halves = [slice(HALF, S), slice(0, HALF)]
+        wx = sb.tile([P, S], F32, name="wx")
+        cp = sb.tile([P, S], F32, name="cp")
+        nc.vector.scalar_tensor_tensor(wx[:], pd[:, :S], 0.2, wts[:], ALU.add, ALU.mult)
+        for h in reversed(halves):
+            nc.vector.tensor_tensor(cp[:, h], sg[:, 1, h], pd[:, h], ALU.mult)
+
+        lg = sb.tile([P, S], F32, name="lg")
+        for c in reversed(range(S // PIECE)):
+            cols = slice(c * PIECE, (c + 1) * PIECE)
+            reach = slice(c * PIECE, min((c + 1) * PIECE + 1, S))
+            nc.scalar.activation(lg[:, reach], sg[:, 0, reach], ACT.Ln, scale=math.exp(-2.0), bias=LN_FLOOR)
+        for c in reversed(range(S // PIECE)):
+            cols = slice(c * PIECE, (c + 1) * PIECE)
+            nc.vector.scalar_tensor_tensor(nf[:, cols], acc[c][:, 0, :], -2.0, lg[:, cols], ALU.add, ALU.min)
+
+        rs = sg[:, 0, :S]
+        nc.scalar.activation(rs, pd[:, :S], ACT.Abs_reciprocal_sqrt, bias=0.2)
+        inv = sb.tile([P, S], F32, name="inv")
+        for h in halves:
+            nc.scalar.activation(inv[:, h], sg[:, 0, h], ACT.Square)
+
+        mm = sb.tile([P, S], F32, name="mm")
+        t2 = sb.tile([P, S], F32, name="t2")
+        dd = sb.tile([P, S], F32, name="dd")
+        ee = sb.tile([P, S], F32, name="ee")
+        uu = sb.tile([P, S], F32, name="uu")
+        u2 = sb.tile([P, S], F32, name="u2")
+        t1 = sb.tile([P, S], F32, name="t1")
+        res = sb.tile([P, S], F32, name="res")
+
+        def shifted(h, by):
+            return slice(h.start + by, h.stop + by)
+
+        for h in halves:
+            nc.vector.tensor_tensor(qq[:, h], nf[:, h], nf[:, shifted(h, 1)], ALU.mult)
+        for h in halves:
+            nc.vector.scalar_tensor_tensor(dd[:, h], nf[:, h], half[:], pd[:, h], ALU.mult, ALU.mult)
+        for h in halves:
+            nc.vector.scalar_tensor_tensor(mm[:, h], qq[:, shifted(h, 2)], 4.0, cp[:, h], ALU.max, ALU.mult)
+        for h in halves:
+            nc.vector.tensor_tensor(ee[:, h], dd[:, h], pd[:, shifted(h, 1)], ALU.add)
+        for h in halves:
+            nc.vector.tensor_tensor(uu[:, h], ee[:, h], inv[:, h], ALU.mult)
+            nc.scalar.activation(u2[:, h], uu[:, h], ACT.Square)
+        for h in halves:
+            nc.vector.scalar_tensor_tensor(t2[:, h], qq[:, h], 1.0 / 16.0, mm[:, h], ALU.mult, ALU.mult)
+        for h in halves:
+            nc.vector.tensor_tensor(t1[:, h], u2[:, h], wx[:, h], ALU.mult)
+        for h in halves:
+            nc.vector.tensor_tensor(res[:, h], t1[:, h], t2[:, h], ALU.add)
+            nc.sync.dma_start(out=out[:, h], in_=res[:, h])

@@ -34,9 +34,9 @@ def tile_picked_ychnld_err_p_kernel(tc, x_words, x_scales, w1, w2, paid, wt, off
         nc.sync.dma_start(offsets[:], offs)
 
         xs = sb.tile([P, T], U8, name="xs", align_bytes=64)
-        nc.vector.memset(xs[:].bitcast(I32), 0)
+        nc.gpsimd.memset(xs[:].bitcast(I32), 0)
         for q in range(4):
-            nc.scalar.dma_start(out=xs[32 * q : 32 * q + 4, :].bitcast(I32), in_=x_scales[0, 4 * q : 4 * q + 4, :].bitcast(I32))
+            nc.sync.dma_start(out=xs[32 * q : 32 * q + 4, :].bitcast(I32), in_=x_scales[0, 4 * q : 4 * q + 4, :].bitcast(I32))
 
         w_raw = []
         for i, w in enumerate((w1, w2)):
@@ -47,12 +47,13 @@ def tile_picked_ychnld_err_p_kernel(tc, x_words, x_scales, w1, w2, paid, wt, off
         xw = sb.tile([P, T], U32, name="xw", align_bytes=64)
         nc.sync.dma_start(out=xw[:].bitcast(I32), in_=x_words[0].rearrange("p n t -> p (n t)").bitcast(I32))
 
-        pd = sb.tile([P, S + PAD], F32, name="pd")
+        pw = sb.tile([P, 2, S + PAD], F32, name="pw")
+        nc.vector.memset(pw[:, :, S - PAD :], 0.0)
+        pd = pw[:, 0, :]
+        wts = pw[:, 1, :S]
         nc.sync.dma_start(out=pd[:, :S], in_=paid)
-        wts = sb.tile([P, S], F32, name="wts")
-        nc.sync.dma_start(out=wts[:], in_=wt)
+        nc.sync.dma_start(out=wts, in_=wt)
 
-        nc.vector.memset(pd[:, S:], 0.0)
         half = sb.tile([P, 1], F32, name="half")
         nc.scalar.activation(half[:], pd[:, S : S + 1], ACT.Sigmoid)
 
@@ -66,48 +67,55 @@ def tile_picked_ychnld_err_p_kernel(tc, x_words, x_scales, w1, w2, paid, wt, off
             nc.scalar.activation(w_bf[:, i], w_raw[i][:].rearrange("p j m -> p m j"), ACT.Copy, scale=sign)
 
         gs = sb.tile([P, S], U8, name="gs", align_bytes=64)
-        for h in range(S // HALF):
-            nc.vector.tensor_copy(gs[:, h * HALF : (h + 1) * HALF], xs[:].indirect(offsets[:, h * HALF // 16 : (h + 1) * HALF // 16]))
+        nc.vector.tensor_copy(gs[:], xs[:].indirect(offsets[:]))
 
         w_codes = sb.tile([P, 2 * M], U32, name="w_codes", align_bytes=64)
         w_scales = sb.tile([P, 2 * M], U8, name="w_scales", align_bytes=64)
         nc.vector.quantize_mx(out=w_codes[:].bitcast(FP8X4), scales=w_scales[:], in_=w_bf[:].rearrange("p i m j -> p (i m j)"))
 
         sg = sb.tile([P, 2, S + PAD], F32, name="sg")
-        acc = []
-        for c in range(S // PIECE):
+        acc = {}
+        order = (0, 1, 3, 2)
+        for c in order:
             cols = slice(c * PIECE, (c + 1) * PIECE)
             gw = sb.tile([P, PIECE], U32, name="gw%d" % c, align_bytes=64)
             nc.vector.tensor_copy(gw[:], xw[:].indirect(offsets[:, c * PIECE // 16 : (c + 1) * PIECE // 16]))
-            bank = ps.tile([P, 2, PIECE], F32, name="bank%d" % c)
-            for i in range(2):
-                nc.tensor.matmul_mx(
-                    out=bank[:, i, :],
-                    lhsT=w_codes[:, i * M : (i + 1) * M].bitcast(FP8X4),
-                    lhsT_scale=w_scales[:, i * M : (i + 1) * M],
-                    rhs=gw[:].bitcast(FP8X4),
-                    rhs_scale=gs[:, cols],
-                    start=True,
-                    stop=True,
-                )
-            nc.scalar.activation(sg[:, :, cols], bank[:], ACT.Sigmoid)
-            acc.append(bank)
+            if c != order[-1]:
+                bank = ps.tile([P, 2, PIECE], F32, name="bank%d" % c)
+                groups = [(bank, (0, 1))]
+            else:
+                bank = ps.tile([P, 1, PIECE], F32, name="bank%d" % c)
+                other = ps.tile([P, 1, PIECE], F32, name="other")
+                groups = [(other, (1,)), (bank, (0,))]
+            for tile, which in groups:
+                for i in which:
+                    nc.tensor.matmul_mx(
+                        out=tile[:, i - which[0], :],
+                        lhsT=w_codes[:, i * M : (i + 1) * M].bitcast(FP8X4),
+                        lhsT_scale=w_scales[:, i * M : (i + 1) * M],
+                        rhs=gw[:].bitcast(FP8X4),
+                        rhs_scale=gs[:, cols],
+                        start=True,
+                        stop=True,
+                    )
+                nc.scalar.activation(sg[:, which[0] : which[-1] + 1, cols], tile[:], ACT.Sigmoid)
+            acc[c] = bank
 
         halves = [slice(HALF, S), slice(0, HALF)]
         wx = sb.tile([P, S], F32, name="wx")
         cp = sb.tile([P, S], F32, name="cp")
-        nc.vector.scalar_tensor_tensor(wx[:], pd[:, :S], 0.2, wts[:], ALU.add, ALU.mult)
+        nc.vector.scalar_tensor_tensor(wx[:], pd[:, :S], 0.2, wts, ALU.add, ALU.mult)
         for h in reversed(halves):
             nc.vector.tensor_tensor(cp[:, h], sg[:, 1, h], pd[:, h], ALU.mult)
 
-        lg = sb.tile([P, S], F32, name="lg")
-        for c in reversed(range(S // PIECE)):
-            cols = slice(c * PIECE, (c + 1) * PIECE)
-            reach = slice(c * PIECE, min((c + 1) * PIECE + 1, S))
-            nc.scalar.activation(lg[:, reach], sg[:, 0, reach], ACT.Ln, scale=math.exp(-2.0), bias=LN_FLOOR)
-        for c in reversed(range(S // PIECE)):
-            cols = slice(c * PIECE, (c + 1) * PIECE)
-            nc.vector.scalar_tensor_tensor(nf[:, cols], acc[c][:, 0, :], -2.0, lg[:, cols], ALU.add, ALU.min)
+        last = slice(order[-1] * PIECE, (order[-1] + 1) * PIECE)
+        for reach in (slice(last.stop - 1, S), last, slice(0, last.start + 1)):
+            lg = sb.tile([P, reach.stop - reach.start], F32, name="lg%d" % reach.start)
+            nc.scalar.activation(lg[:], sg[:, 0, reach], ACT.Ln, scale=math.exp(-2.0), bias=LN_FLOOR)
+            for c in reversed(range(-(-reach.start // PIECE), reach.stop // PIECE)):
+                cols = slice(c * PIECE, (c + 1) * PIECE)
+                mine = slice(cols.start - reach.start, cols.stop - reach.start)
+                nc.vector.scalar_tensor_tensor(nf[:, cols], acc[c][:, 0, :], -2.0, lg[:, mine], ALU.add, ALU.min)
 
         rs = sg[:, 0, :S]
         nc.scalar.activation(rs, pd[:, :S], ACT.Abs_reciprocal_sqrt, bias=0.2)
@@ -127,21 +135,19 @@ def tile_picked_ychnld_err_p_kernel(tc, x_words, x_scales, w1, w2, paid, wt, off
         def shifted(h, by):
             return slice(h.start + by, h.stop + by)
 
-        for h in halves:
-            nc.vector.tensor_tensor(qq[:, h], nf[:, h], nf[:, shifted(h, 1)], ALU.mult)
-        for h in halves:
-            nc.vector.scalar_tensor_tensor(dd[:, h], nf[:, h], half[:], pd[:, h], ALU.mult, ALU.mult)
-        for h in halves:
-            nc.vector.scalar_tensor_tensor(mm[:, h], qq[:, shifted(h, 2)], 4.0, cp[:, h], ALU.max, ALU.mult)
-        for h in halves:
-            nc.vector.tensor_tensor(ee[:, h], dd[:, h], pd[:, shifted(h, 1)], ALU.add)
+        hi, lo = halves
+        whole = slice(0, S)
+        nc.vector.scalar_tensor_tensor(dd[:, hi], nf[:, hi], half[:], pd[:, hi], ALU.mult, ALU.mult)
+        nc.vector.tensor_tensor(qq[:, whole], nf[:, whole], nf[:, shifted(whole, 1)], ALU.mult)
+        nc.vector.scalar_tensor_tensor(dd[:, lo], nf[:, lo], half[:], pd[:, lo], ALU.mult, ALU.mult)
+        nc.vector.scalar_tensor_tensor(mm[:], qq[:, shifted(whole, 2)], 4.0, cp[:], ALU.max, ALU.mult)
+        nc.vector.tensor_tensor(ee[:], dd[:], pd[:, shifted(whole, 1)], ALU.add)
+        nc.vector.scalar_tensor_tensor(t2[:], qq[:, whole], 1.0 / 16.0, mm[:], ALU.mult, ALU.mult)
         for h in halves:
             nc.vector.tensor_tensor(uu[:, h], ee[:, h], inv[:, h], ALU.mult)
             nc.scalar.activation(u2[:, h], uu[:, h], ACT.Square)
         for h in halves:
-            nc.vector.scalar_tensor_tensor(t2[:, h], qq[:, h], 1.0 / 16.0, mm[:, h], ALU.mult, ALU.mult)
-        for h in halves:
             nc.vector.tensor_tensor(t1[:, h], u2[:, h], wx[:, h], ALU.mult)
-        for h in halves:
+        for h, queue in ((hi, nc.sync), (slice(PIECE, HALF), nc.scalar), (slice(0, PIECE), nc.sync)):
             nc.vector.tensor_tensor(res[:, h], t1[:, h], t2[:, h], ALU.add)
-            nc.sync.dma_start(out=out[:, h], in_=res[:, h])
+            queue.dma_start(out=out[:, h], in_=res[:, h])

@@ -18,10 +18,15 @@ ACT = mybir.ActivationFunctionType
 
 P = 128
 PACK = 4
+GROUP = 16
 PIECE = 256
-HALF = 512
+HALF = S // 2
 PAD = 8
-LN_FLOOR = 2.0 ** -62
+LN_FLOOR = 2.0**-62
+
+
+def shifted(cols, by):
+    return slice(cols.start + by, cols.stop + by)
 
 
 def tile_picked_ychnld_err_p_kernel(tc, x_words, x_scales, w1, w2, paid, wt, offs, out):
@@ -30,13 +35,16 @@ def tile_picked_ychnld_err_p_kernel(tc, x_words, x_scales, w1, w2, paid, wt, off
         sb = ctx.enter_context(tc.tile_pool(name="sb", bufs=1))
         ps = ctx.enter_context(tc.psum_pool(name="ps", bufs=1))
 
-        offsets = sb.tile([P, S // 16], U16, name="offsets")
+        offsets = sb.tile([P, S // GROUP], U16, name="offsets")
         nc.sync.dma_start(offsets[:], offs)
 
-        xs = sb.tile([P, T], U8, name="xs", align_bytes=64)
-        nc.gpsimd.memset(xs[:].bitcast(I32), 0)
+        x_scale_table = sb.tile([P, T], U8, name="x_scale_table", align_bytes=64)
+        nc.gpsimd.memset(x_scale_table[:].bitcast(I32), 0)
         for q in range(4):
-            nc.sync.dma_start(out=xs[32 * q : 32 * q + 4, :].bitcast(I32), in_=x_scales[0, 4 * q : 4 * q + 4, :].bitcast(I32))
+            nc.sync.dma_start(
+                out=x_scale_table[32 * q : 32 * q + 4, :].bitcast(I32),
+                in_=x_scales[0, 4 * q : 4 * q + 4, :].bitcast(I32),
+            )
 
         w_raw = []
         for i, w in enumerate((w1, w2)):
@@ -44,110 +52,104 @@ def tile_picked_ychnld_err_p_kernel(tc, x_words, x_scales, w1, w2, paid, wt, off
             nc.sync.dma_start(out=raw[:], in_=w.rearrange("(p j) m -> p j m", j=PACK))
             w_raw.append(raw)
 
-        xw = sb.tile([P, T], U32, name="xw", align_bytes=64)
-        nc.sync.dma_start(out=xw[:].bitcast(I32), in_=x_words[0].rearrange("p n t -> p (n t)").bitcast(I32))
+        x_word_table = sb.tile([P, T], U32, name="x_word_table", align_bytes=64)
+        nc.sync.dma_start(out=x_word_table[:].bitcast(I32), in_=x_words[0].rearrange("p n t -> p (n t)").bitcast(I32))
 
-        pw = sb.tile([P, 2, S + PAD], F32, name="pw")
-        nc.vector.memset(pw[:, :, S - PAD :], 0.0)
-        pd = pw[:, 0, :]
-        wts = pw[:, 1, :S]
-        nc.sync.dma_start(out=pd[:, :S], in_=paid)
-        nc.sync.dma_start(out=wts, in_=wt)
+        paid_wt = sb.tile([P, 2, S + PAD], F32, name="paid_wt")
+        nc.vector.memset(paid_wt[:, :, S - PAD :], 0.0)
+        pay = paid_wt[:, 0, :]
+        weight = paid_wt[:, 1, :S]
+        nc.sync.dma_start(out=pay[:, :S], in_=paid)
+        nc.sync.dma_start(out=weight, in_=wt)
 
         half = sb.tile([P, 1], F32, name="half")
-        nc.scalar.activation(half[:], pd[:, S : S + 1], ACT.Sigmoid)
+        nc.scalar.activation(half[:], pay[:, S : S + 1], ACT.Sigmoid)
 
-        nf = sb.tile([P, S + PAD], F32, name="nf")
-        qq = sb.tile([P, S + PAD], F32, name="qq")
-        nc.vector.memset(nf[:, S:], 0.0)
-        nc.vector.memset(qq[:, S:], 0.0)
+        neg2fac = sb.tile([P, S + PAD], F32, name="neg2fac")
+        fac2x4 = sb.tile([P, S + PAD], F32, name="fac2x4")
+        nc.vector.memset(neg2fac[:, S:], 0.0)
+        nc.vector.memset(fac2x4[:, S:], 0.0)
 
-        w_bf = sb.tile([P, 2, M, PACK], BF16, name="w_bf", align_bytes=64)
+        w_bf16 = sb.tile([P, 2, M, PACK], BF16, name="w_bf16", align_bytes=64)
         for i, sign in enumerate((-1.0, 1.0)):
-            nc.scalar.activation(w_bf[:, i], w_raw[i][:].rearrange("p j m -> p m j"), ACT.Copy, scale=sign)
+            nc.scalar.activation(w_bf16[:, i], w_raw[i][:].rearrange("p j m -> p m j"), ACT.Copy, scale=sign)
 
-        gs = sb.tile([P, S], U8, name="gs", align_bytes=64)
-        nc.vector.tensor_copy(gs[:], xs[:].indirect(offsets[:]))
+        x_scales_picked = sb.tile([P, S], U8, name="x_scales_picked", align_bytes=64)
+        nc.vector.tensor_copy(x_scales_picked[:], x_scale_table[:].indirect(offsets[:]))
 
         w_codes = sb.tile([P, 2 * M], U32, name="w_codes", align_bytes=64)
         w_scales = sb.tile([P, 2 * M], U8, name="w_scales", align_bytes=64)
-        nc.vector.quantize_mx(out=w_codes[:].bitcast(FP8X4), scales=w_scales[:], in_=w_bf[:].rearrange("p i m j -> p (i m j)"))
+        nc.vector.quantize_mx(
+            out=w_codes[:].bitcast(FP8X4), scales=w_scales[:], in_=w_bf16[:].rearrange("p i m j -> p (i m j)")
+        )
 
-        sg = sb.tile([P, 2, S + PAD], F32, name="sg")
-        acc = {}
+        sig = sb.tile([P, 2, S], F32, name="sig")
+        z_bank = {}
         order = (0, 1, 3, 2)
         for c in order:
             cols = slice(c * PIECE, (c + 1) * PIECE)
-            gw = sb.tile([P, PIECE], U32, name="gw%d" % c, align_bytes=64)
-            nc.vector.tensor_copy(gw[:], xw[:].indirect(offsets[:, c * PIECE // 16 : (c + 1) * PIECE // 16]))
-            if c != order[-1]:
-                bank = ps.tile([P, 2, PIECE], F32, name="bank%d" % c)
-                groups = [(bank, (0, 1))]
-            else:
-                bank = ps.tile([P, 1, PIECE], F32, name="bank%d" % c)
-                other = ps.tile([P, 1, PIECE], F32, name="other")
-                groups = [(other, (1,)), (bank, (0,))]
-            for tile, which in groups:
-                for i in which:
+            words = sb.tile([P, PIECE], U32, name="words%d" % c, align_bytes=64)
+            nc.vector.tensor_copy(words[:], x_word_table[:].indirect(offsets[:, cols.start // GROUP : cols.stop // GROUP]))
+            for products in ((0, 1),) if c != order[-1] else ((1,), (0,)):
+                bank = ps.tile([P, len(products), PIECE], F32, name="bank%d_%d" % (c, products[0]))
+                for i in products:
                     nc.tensor.matmul_mx(
-                        out=tile[:, i - which[0], :],
+                        out=bank[:, i - products[0], :],
                         lhsT=w_codes[:, i * M : (i + 1) * M].bitcast(FP8X4),
                         lhsT_scale=w_scales[:, i * M : (i + 1) * M],
-                        rhs=gw[:].bitcast(FP8X4),
-                        rhs_scale=gs[:, cols],
+                        rhs=words[:].bitcast(FP8X4),
+                        rhs_scale=x_scales_picked[:, cols],
                         start=True,
                         stop=True,
                     )
-                nc.scalar.activation(sg[:, which[0] : which[-1] + 1, cols], tile[:], ACT.Sigmoid)
-            acc[c] = bank
+                nc.scalar.activation(sig[:, products[0] : products[-1] + 1, cols], bank[:], ACT.Sigmoid)
+            z_bank[c] = bank
 
-        halves = [slice(HALF, S), slice(0, HALF)]
-        wx = sb.tile([P, S], F32, name="wx")
-        cp = sb.tile([P, S], F32, name="cp")
-        nc.vector.scalar_tensor_tensor(wx[:], pd[:, :S], 0.2, wts, ALU.add, ALU.mult)
-        for h in reversed(halves):
-            nc.vector.tensor_tensor(cp[:, h], sg[:, 1, h], pd[:, h], ALU.mult)
+        hi, lo, whole = slice(HALF, S), slice(0, HALF), slice(0, S)
+        weight_x = sb.tile([P, S], F32, name="weight_x")
+        cred_pay = sb.tile([P, S], F32, name="cred_pay")
+        nc.vector.scalar_tensor_tensor(weight_x[:], pay[:, whole], 0.2, weight, ALU.add, ALU.mult)
+        for h in (lo, hi):
+            nc.vector.tensor_tensor(cred_pay[:, h], sig[:, 1, h], pay[:, h], ALU.mult)
 
         last = slice(order[-1] * PIECE, (order[-1] + 1) * PIECE)
         for reach in (slice(last.stop - 1, S), last, slice(0, last.start + 1)):
-            lg = sb.tile([P, reach.stop - reach.start], F32, name="lg%d" % reach.start)
-            nc.scalar.activation(lg[:], sg[:, 0, reach], ACT.Ln, scale=math.exp(-2.0), bias=LN_FLOOR)
-            for c in reversed(range(-(-reach.start // PIECE), reach.stop // PIECE)):
+            log_sig = sb.tile([P, reach.stop - reach.start], F32, name="log_sig%d" % reach.start)
+            nc.scalar.activation(log_sig[:], sig[:, 0, reach], ACT.Ln, scale=math.exp(-2.0), bias=LN_FLOOR)
+            for c in reversed(range(math.ceil(reach.start / PIECE), reach.stop // PIECE)):
                 cols = slice(c * PIECE, (c + 1) * PIECE)
-                mine = slice(cols.start - reach.start, cols.stop - reach.start)
-                nc.vector.scalar_tensor_tensor(nf[:, cols], acc[c][:, 0, :], -2.0, lg[:, mine], ALU.add, ALU.min)
+                nc.vector.scalar_tensor_tensor(
+                    neg2fac[:, cols], z_bank[c][:, 0, :], -2.0, log_sig[:, shifted(cols, -reach.start)], ALU.add, ALU.min
+                )
 
-        rs = sg[:, 0, :S]
-        nc.scalar.activation(rs, pd[:, :S], ACT.Abs_reciprocal_sqrt, bias=0.2)
-        inv = sb.tile([P, S], F32, name="inv")
-        for h in halves:
-            nc.scalar.activation(inv[:, h], sg[:, 0, h], ACT.Square)
+        inv_root = sig[:, 0, :]
+        nc.scalar.activation(inv_root, pay[:, whole], ACT.Abs_reciprocal_sqrt, bias=0.2)
+        inv_abs = sb.tile([P, S], F32, name="inv_abs")
+        for h in (hi, lo):
+            nc.scalar.activation(inv_abs[:, h], inv_root[:, h], ACT.Square)
 
-        mm = sb.tile([P, S], F32, name="mm")
-        t2 = sb.tile([P, S], F32, name="t2")
-        dd = sb.tile([P, S], F32, name="dd")
-        ee = sb.tile([P, S], F32, name="ee")
-        uu = sb.tile([P, S], F32, name="uu")
-        u2 = sb.tile([P, S], F32, name="u2")
-        t1 = sb.tile([P, S], F32, name="t1")
-        res = sb.tile([P, S], F32, name="res")
+        neg_pay_fac = sb.tile([P, S], F32, name="neg_pay_fac")
+        err = sb.tile([P, S], F32, name="err")
+        err_rel = sb.tile([P, S], F32, name="err_rel")
+        err_rel_sq = sb.tile([P, S], F32, name="err_rel_sq")
+        err_term = sb.tile([P, S], F32, name="err_term")
+        ahead = sb.tile([P, S], F32, name="ahead")
+        ult_term = sb.tile([P, S], F32, name="ult_term")
+        result = sb.tile([P, S], F32, name="result")
 
-        def shifted(h, by):
-            return slice(h.start + by, h.stop + by)
+        nc.vector.scalar_tensor_tensor(neg_pay_fac[:, hi], neg2fac[:, hi], half[:], pay[:, hi], ALU.mult, ALU.mult)
+        nc.vector.tensor_tensor(fac2x4[:, whole], neg2fac[:, whole], neg2fac[:, shifted(whole, 1)], ALU.mult)
+        nc.vector.scalar_tensor_tensor(neg_pay_fac[:, lo], neg2fac[:, lo], half[:], pay[:, lo], ALU.mult, ALU.mult)
+        nc.vector.tensor_tensor(err[:, hi], neg_pay_fac[:, hi], pay[:, shifted(hi, 1)], ALU.add)
+        nc.vector.scalar_tensor_tensor(ahead[:], fac2x4[:, shifted(whole, 2)], 4.0, cred_pay[:], ALU.max, ALU.mult)
+        nc.vector.tensor_tensor(err[:, lo], neg_pay_fac[:, lo], pay[:, shifted(lo, 1)], ALU.add)
+        for h in (hi, lo):
+            nc.vector.tensor_tensor(err_rel[:, h], err[:, h], inv_abs[:, h], ALU.mult)
+            nc.scalar.activation(err_rel_sq[:, h], err_rel[:, h], ACT.Square)
+        nc.vector.scalar_tensor_tensor(ult_term[:], fac2x4[:, whole], 1.0 / 16.0, ahead[:], ALU.mult, ALU.mult)
+        for h in (hi, lo):
+            nc.vector.tensor_tensor(err_term[:, h], err_rel_sq[:, h], weight_x[:, h], ALU.mult)
 
-        hi, lo = halves
-        whole = slice(0, S)
-        nc.vector.scalar_tensor_tensor(dd[:, hi], nf[:, hi], half[:], pd[:, hi], ALU.mult, ALU.mult)
-        nc.vector.tensor_tensor(qq[:, whole], nf[:, whole], nf[:, shifted(whole, 1)], ALU.mult)
-        nc.vector.scalar_tensor_tensor(dd[:, lo], nf[:, lo], half[:], pd[:, lo], ALU.mult, ALU.mult)
-        nc.vector.scalar_tensor_tensor(mm[:], qq[:, shifted(whole, 2)], 4.0, cp[:], ALU.max, ALU.mult)
-        nc.vector.tensor_tensor(ee[:], dd[:], pd[:, shifted(whole, 1)], ALU.add)
-        nc.vector.scalar_tensor_tensor(t2[:], qq[:, whole], 1.0 / 16.0, mm[:], ALU.mult, ALU.mult)
-        for h in halves:
-            nc.vector.tensor_tensor(uu[:, h], ee[:, h], inv[:, h], ALU.mult)
-            nc.scalar.activation(u2[:, h], uu[:, h], ACT.Square)
-        for h in halves:
-            nc.vector.tensor_tensor(t1[:, h], u2[:, h], wx[:, h], ALU.mult)
-        for h, queue in ((hi, nc.sync), (slice(PIECE, HALF), nc.scalar), (slice(0, PIECE), nc.sync)):
-            nc.vector.tensor_tensor(res[:, h], t1[:, h], t2[:, h], ALU.add)
-            queue.dma_start(out=out[:, h], in_=res[:, h])
+        for cols, queue in ((hi, nc.sync), (slice(PIECE, HALF), nc.scalar), (slice(0, PIECE), nc.sync)):
+            nc.vector.tensor_tensor(result[:, cols], err_term[:, cols], ult_term[:, cols], ALU.add)
+            queue.dma_start(out=out[:, cols], in_=result[:, cols])

@@ -40,11 +40,8 @@ def tile_picked_ychnld_err_p_kernel(tc, x_words, x_scales, w1, w2, paid, wt, off
 
         x_scale_table = sb.tile([P, T], U8, name="x_scale_table", align_bytes=64)
         nc.gpsimd.memset(x_scale_table[:].bitcast(I32), 0)
-        for q in range(4):
-            nc.sync.dma_start(
-                out=x_scale_table[32 * q : 32 * q + 4, :].bitcast(I32),
-                in_=x_scales[0, 4 * q : 4 * q + 4, :].bitcast(I32),
-            )
+        for r in range(4):
+            nc.sync.dma_start(out=x_scale_table[r:P:32, :].bitcast(I32), in_=x_scales[0, r:16:4, :].bitcast(I32))
 
         w_raw = []
         for i, w in enumerate((w1, w2)):

@@ -2,6 +2,7 @@ import math
 from contextlib import ExitStack
 
 import concourse.mybir as mybir
+from concourse.masks import make_identity
 
 K, T, S, M = 512, 2048, 1024, 128
 FLOPS = 2 * 2 * K * M * S
@@ -62,6 +63,9 @@ def tile_picked_ychnld_err_p_kernel(tc, x_words, x_scales, w1, w2, paid, wt, off
         half = sb.tile([P, 1], F32, name="half")
         nc.scalar.activation(half[:], pay[:, S : S + 1], ACT.Sigmoid)
 
+        identity = sb.tile([P, P], F32, name="identity")
+        make_identity(nc, identity[:])
+
         neg2fac = sb.tile([P, S + PAD], F32, name="neg2fac")
         fac2x4 = sb.tile([P, S + PAD], F32, name="fac2x4")
         nc.vector.memset(neg2fac[:, S:], 0.0)
@@ -82,13 +86,13 @@ def tile_picked_ychnld_err_p_kernel(tc, x_words, x_scales, w1, w2, paid, wt, off
 
         sig = sb.tile([P, 2, S], F32, name="sig")
         z_bank = {}
-        order = (0, 1, 3, 2)
+        order = (0, 2, 3, 1)
         for c in order:
             cols = slice(c * PIECE, (c + 1) * PIECE)
             words = sb.tile([P, PIECE], U32, name="words%d" % c, align_bytes=64)
             nc.vector.tensor_copy(words[:], x_word_table[:].indirect(offsets[:, cols.start // GROUP : cols.stop // GROUP]))
-            for products in ((0, 1),) if c != order[-1] else ((1,), (0,)):
-                bank = ps.tile([P, len(products), PIECE], F32, name="bank%d_%d" % (c, products[0]))
+            for products in ((0, 1),) if c in order[:2] else ((1,), (0,)):
+                bank = ps.tile([P, len(products), PIECE], F32, name="bank", tag="bank%d_%d" % (c, products[0]))
                 for i in products:
                     nc.tensor.matmul_mx(
                         out=bank[:, i - products[0], :],
@@ -103,11 +107,23 @@ def tile_picked_ychnld_err_p_kernel(tc, x_words, x_scales, w1, w2, paid, wt, off
             z_bank[c] = bank
 
         hi, lo, whole = slice(HALF, S), slice(0, HALF), slice(0, S)
+        pay_psum = {}
+        for h, freed in ((hi, "bank%d_1" % order[-2]), (lo, "bank%d_1" % order[-1])):
+            turned = ps.tile([P, HALF], F32, name="turned", tag=freed)
+            for b in range(0, HALF, P):
+                nc.tensor.transpose(turned[:, b : b + P], pay[:, h.start + b : h.start + b + P], identity[:])
+            turned_sb = sb.tile([P, HALF], F32, name="turned_sb%d" % h.start)
+            nc.vector.tensor_copy(turned_sb[:], turned[:])
+            back = ps.tile([P, HALF], F32, name="back%d" % h.start)
+            for b in range(0, HALF, P):
+                nc.tensor.transpose(back[:, b : b + P], turned_sb[:, b : b + P], identity[:])
+            pay_psum[h.start] = back
+
         weight_x = sb.tile([P, S], F32, name="weight_x")
-        cred_pay = sb.tile([P, S], F32, name="cred_pay")
+        half_cred_pay = sb.tile([P, S], F32, name="half_cred_pay")
         nc.vector.scalar_tensor_tensor(weight_x[:], pay[:, whole], 0.2, weight, ALU.add, ALU.mult)
-        for h in (lo, hi):
-            nc.vector.tensor_tensor(cred_pay[:, h], sig[:, 1, h], pay[:, h], ALU.mult)
+        for h in (hi, lo):
+            nc.vector.scalar_tensor_tensor(half_cred_pay[:, h], sig[:, 1, h], half[:], pay[:, h], ALU.mult, ALU.mult)
 
         last = slice(order[-1] * PIECE, (order[-1] + 1) * PIECE)
         for reach in (slice(last.stop - 1, S), last, slice(0, last.start + 1)):
@@ -130,20 +146,26 @@ def tile_picked_ychnld_err_p_kernel(tc, x_words, x_scales, w1, w2, paid, wt, off
         err_rel = sb.tile([P, S], F32, name="err_rel")
         err_rel_sq = sb.tile([P, S], F32, name="err_rel_sq")
         err_term = sb.tile([P, S], F32, name="err_term")
-        ahead = sb.tile([P, S], F32, name="ahead")
         ult_term = sb.tile([P, S], F32, name="ult_term")
         result = sb.tile([P, S], F32, name="result")
 
-        nc.vector.scalar_tensor_tensor(neg_pay_fac[:, hi], neg2fac[:, hi], half[:], pay[:, hi], ALU.mult, ALU.mult)
-        nc.vector.tensor_tensor(fac2x4[:, whole], neg2fac[:, whole], neg2fac[:, shifted(whole, 1)], ALU.mult)
-        nc.vector.scalar_tensor_tensor(neg_pay_fac[:, lo], neg2fac[:, lo], half[:], pay[:, lo], ALU.mult, ALU.mult)
-        nc.vector.tensor_tensor(err[:, hi], neg_pay_fac[:, hi], pay[:, shifted(hi, 1)], ALU.add)
-        nc.vector.scalar_tensor_tensor(ahead[:], fac2x4[:, shifted(whole, 2)], 4.0, cred_pay[:], ALU.max, ALU.mult)
-        nc.vector.tensor_tensor(err[:, lo], neg_pay_fac[:, lo], pay[:, shifted(lo, 1)], ALU.add)
+        for h in (hi, lo):
+            nc.gpsimd.tensor_tensor(fac2x4[:, h], neg2fac[:, h], neg2fac[:, shifted(h, 1)], ALU.mult)
+        for h in (hi, lo):
+            nc.vector.scalar_tensor_tensor(neg_pay_fac[:, h], pay_psum[h.start][:], 0.5, neg2fac[:, h], ALU.mult, ALU.mult)
+        nc.vector.tensor_copy(err[:, S - 1 :], neg_pay_fac[:, S - 1 :])
+        for cols, next_pay in (
+            (slice(HALF, S - 1), pay_psum[HALF][:, 1:]),
+            (slice(HALF - 1, HALF), pay_psum[HALF][:, :1]),
+            (slice(0, HALF - 1), pay_psum[0][:, 1:]),
+        ):
+            nc.vector.tensor_tensor(err[:, cols], next_pay, neg_pay_fac[:, cols], ALU.add)
+        ahead = neg_pay_fac
+        nc.vector.scalar_tensor_tensor(ahead[:], fac2x4[:, shifted(whole, 2)], 4.0, half_cred_pay[:], ALU.max, ALU.mult)
         for h in (hi, lo):
             nc.vector.tensor_tensor(err_rel[:, h], err[:, h], inv_abs[:, h], ALU.mult)
             nc.scalar.activation(err_rel_sq[:, h], err_rel[:, h], ACT.Square)
-        nc.vector.scalar_tensor_tensor(ult_term[:], fac2x4[:, whole], 1.0 / 16.0, ahead[:], ALU.mult, ALU.mult)
+        nc.vector.scalar_tensor_tensor(ult_term[:], fac2x4[:, whole], 1.0 / 8.0, ahead[:], ALU.mult, ALU.mult)
         for h in (hi, lo):
             nc.vector.tensor_tensor(err_term[:, h], err_rel_sq[:, h], weight_x[:, h], ALU.mult)
 

import math
from contextlib import ExitStack

import concourse.mybir as mybir
from concourse.masks import make_identity

K, T, S, M = 512, 2048, 1024, 128
FLOPS = 2 * 2 * K * M * S

F32 = mybir.dt.float32
BF16 = mybir.dt.bfloat16
I32 = mybir.dt.int32
U32 = mybir.dt.uint32
U16 = mybir.dt.uint16
U8 = mybir.dt.uint8
FP8X4 = mybir.dt.float8_e4m3fn_x4
ALU = mybir.AluOpType
ACT = mybir.ActivationFunctionType

P = 128
PACK = 4
GROUP = 16
PIECE = 256
HALF = S // 2
PAD = 8
LN_FLOOR = 2.0**-62


def shifted(cols, by):
    return slice(cols.start + by, cols.stop + by)


def tile_picked_ychnld_err_p_kernel(tc, x_words, x_scales, w1, w2, paid, wt, offs, out):
    nc = tc.nc
    with ExitStack() as ctx:
        sb = ctx.enter_context(tc.tile_pool(name="sb", bufs=1))
        ps = ctx.enter_context(tc.psum_pool(name="ps", bufs=1))

        offsets = sb.tile([P, S // GROUP], U16, name="offsets")
        nc.sync.dma_start(offsets[:], offs)

        x_scale_table = sb.tile([P, T], U8, name="x_scale_table", align_bytes=64)
        nc.gpsimd.memset(x_scale_table[:].bitcast(I32), 0)
        for r in range(4):
            nc.sync.dma_start(out=x_scale_table[r:P:32, :].bitcast(I32), in_=x_scales[0, r:16:4, :].bitcast(I32))

        w_raw = []
        for i, w in enumerate((w1, w2)):
            raw = sb.tile([P, PACK, M], F32, name="w_raw%d" % i)
            nc.sync.dma_start(out=raw[:], in_=w.rearrange("(p j) m -> p j m", j=PACK))
            w_raw.append(raw)

        x_word_table = sb.tile([P, T], U32, name="x_word_table", align_bytes=64)
        nc.sync.dma_start(out=x_word_table[:].bitcast(I32), in_=x_words[0].rearrange("p n t -> p (n t)").bitcast(I32))

        paid_wt = sb.tile([P, 2, S + PAD], F32, name="paid_wt")
        nc.vector.memset(paid_wt[:, :, S - PAD :], 0.0)
        pay = paid_wt[:, 0, :]
        weight = paid_wt[:, 1, :S]
        nc.sync.dma_start(out=pay[:, :S], in_=paid)
        nc.sync.dma_start(out=weight, in_=wt)

        half = sb.tile([P, 1], F32, name="half")
        nc.scalar.activation(half[:], pay[:, S : S + 1], ACT.Sigmoid)

        identity = sb.tile([P, P], F32, name="identity")
        make_identity(nc, identity[:])

        neg2fac = sb.tile([P, S + PAD], F32, name="neg2fac")
        fac2x4 = sb.tile([P, S + PAD], F32, name="fac2x4")
        nc.vector.memset(neg2fac[:, S:], 0.0)
        nc.vector.memset(fac2x4[:, S:], 0.0)

        w_bf16 = sb.tile([P, 2, M, PACK], BF16, name="w_bf16", align_bytes=64)
        for i, sign in enumerate((-1.0, 1.0)):
            nc.scalar.activation(w_bf16[:, i], w_raw[i][:].rearrange("p j m -> p m j"), ACT.Copy, scale=sign)

        x_scales_picked = sb.tile([P, S], U8, name="x_scales_picked", align_bytes=64)
        nc.vector.tensor_copy(x_scales_picked[:], x_scale_table[:].indirect(offsets[:]))

        w_codes = sb.tile([P, 2 * M], U32, name="w_codes", align_bytes=64)
        w_scales = sb.tile([P, 2 * M], U8, name="w_scales", align_bytes=64)
        nc.vector.quantize_mx(
            out=w_codes[:].bitcast(FP8X4), scales=w_scales[:], in_=w_bf16[:].rearrange("p i m j -> p (i m j)")
        )

        sig = sb.tile([P, 2, S], F32, name="sig")
        z_bank = {}
        order = (0, 2, 3, 1)
        for c in order:
            cols = slice(c * PIECE, (c + 1) * PIECE)
            words = sb.tile([P, PIECE], U32, name="words%d" % c, align_bytes=64)
            nc.vector.tensor_copy(words[:], x_word_table[:].indirect(offsets[:, cols.start // GROUP : cols.stop // GROUP]))
            for products in ((0, 1),) if c in order[:2] else ((1,), (0,)):
                bank = ps.tile([P, len(products), PIECE], F32, name="bank", tag="bank%d_%d" % (c, products[0]))
                for i in products:
                    nc.tensor.matmul_mx(
                        out=bank[:, i - products[0], :],
                        lhsT=w_codes[:, i * M : (i + 1) * M].bitcast(FP8X4),
                        lhsT_scale=w_scales[:, i * M : (i + 1) * M],
                        rhs=words[:].bitcast(FP8X4),
                        rhs_scale=x_scales_picked[:, cols],
                        start=True,
                        stop=True,
                    )
                nc.scalar.activation(sig[:, products[0] : products[-1] + 1, cols], bank[:], ACT.Sigmoid)
            z_bank[c] = bank

        hi, lo, whole = slice(HALF, S), slice(0, HALF), slice(0, S)
        pay_psum = {}
        for h, freed in ((hi, "bank%d_1" % order[-2]), (lo, "bank%d_1" % order[-1])):
            turned = ps.tile([P, HALF], F32, name="turned", tag=freed)
            for b in range(0, HALF, P):
                nc.tensor.transpose(turned[:, b : b + P], pay[:, h.start + b : h.start + b + P], identity[:])
            turned_sb = sb.tile([P, HALF], F32, name="turned_sb%d" % h.start)
            nc.vector.tensor_copy(turned_sb[:], turned[:])
            back = ps.tile([P, HALF], F32, name="back%d" % h.start)
            for b in range(0, HALF, P):
                nc.tensor.transpose(back[:, b : b + P], turned_sb[:, b : b + P], identity[:])
            pay_psum[h.start] = back

        weight_x = sb.tile([P, S], F32, name="weight_x")
        half_cred_pay = sb.tile([P, S], F32, name="half_cred_pay")
        nc.vector.scalar_tensor_tensor(weight_x[:], pay[:, whole], 0.2, weight, ALU.add, ALU.mult)
        for h in (hi, lo):
            nc.vector.scalar_tensor_tensor(half_cred_pay[:, h], sig[:, 1, h], half[:], pay[:, h], ALU.mult, ALU.mult)

        last = slice(order[-1] * PIECE, (order[-1] + 1) * PIECE)
        for reach in (slice(last.stop - 1, S), last, slice(0, last.start + 1)):
            log_sig = sb.tile([P, reach.stop - reach.start], F32, name="log_sig%d" % reach.start)
            nc.scalar.activation(log_sig[:], sig[:, 0, reach], ACT.Ln, scale=math.exp(-2.0), bias=LN_FLOOR)
            for c in reversed(range(math.ceil(reach.start / PIECE), reach.stop // PIECE)):
                cols = slice(c * PIECE, (c + 1) * PIECE)
                nc.vector.scalar_tensor_tensor(
                    neg2fac[:, cols], z_bank[c][:, 0, :], -2.0, log_sig[:, shifted(cols, -reach.start)], ALU.add, ALU.min
                )

        inv_root = sig[:, 0, :]
        nc.scalar.activation(inv_root, pay[:, whole], ACT.Abs_reciprocal_sqrt, bias=0.2)
        inv_abs = sb.tile([P, S], F32, name="inv_abs")
        for h in (hi, lo):
            nc.scalar.activation(inv_abs[:, h], inv_root[:, h], ACT.Square)

        neg_pay_fac = sb.tile([P, S], F32, name="neg_pay_fac")
        err = sb.tile([P, S], F32, name="err")
        err_rel = sb.tile([P, S], F32, name="err_rel")
        err_rel_sq = sb.tile([P, S], F32, name="err_rel_sq")
        err_term = sb.tile([P, S], F32, name="err_term")
        ult_term = sb.tile([P, S], F32, name="ult_term")
        result = sb.tile([P, S], F32, name="result")

        for h in (hi, lo):
            nc.gpsimd.tensor_tensor(fac2x4[:, h], neg2fac[:, h], neg2fac[:, shifted(h, 1)], ALU.mult)
        for h in (hi, lo):
            nc.vector.scalar_tensor_tensor(neg_pay_fac[:, h], pay_psum[h.start][:], 0.5, neg2fac[:, h], ALU.mult, ALU.mult)
        nc.vector.tensor_copy(err[:, S - 1 :], neg_pay_fac[:, S - 1 :])
        for cols, next_pay in (
            (slice(HALF, S - 1), pay_psum[HALF][:, 1:]),
            (slice(HALF - 1, HALF), pay_psum[HALF][:, :1]),
            (slice(0, HALF - 1), pay_psum[0][:, 1:]),
        ):
            nc.vector.tensor_tensor(err[:, cols], next_pay, neg_pay_fac[:, cols], ALU.add)
        ahead = neg_pay_fac
        nc.vector.scalar_tensor_tensor(ahead[:], fac2x4[:, shifted(whole, 2)], 4.0, half_cred_pay[:], ALU.max, ALU.mult)
        for h in (hi, lo):
            nc.vector.tensor_tensor(err_rel[:, h], err[:, h], inv_abs[:, h], ALU.mult)
            nc.scalar.activation(err_rel_sq[:, h], err_rel[:, h], ACT.Square)
        nc.vector.scalar_tensor_tensor(ult_term[:], fac2x4[:, whole], 1.0 / 8.0, ahead[:], ALU.mult, ALU.mult)
        for h in (hi, lo):
            nc.vector.tensor_tensor(err_term[:, h], err_rel_sq[:, h], weight_x[:, h], ALU.mult)

        for cols, queue in ((hi, nc.sync), (slice(PIECE, HALF), nc.scalar), (slice(0, PIECE), nc.sync)):
            nc.vector.tensor_tensor(result[:, cols], err_term[:, cols], ult_term[:, cols], ALU.add)
            queue.dma_start(out=out[:, cols], in_=result[:, cols])
